import numpy as np
import ml_dtypes


def mxq(x, axis, fmt="e4m3"):
    dtype, down = {"e4m3": (ml_dtypes.float8_e4m3fn, 7), "e5m2": (ml_dtypes.float8_e5m2, 14)}[fmt]
    v = np.moveaxis(np.asarray(x, np.float32).astype(ml_dtypes.bfloat16).astype(np.float64), axis, -1)
    blocks = v.reshape(v.shape[:-1] + (-1, 32))
    amax = np.abs(blocks).max(-1, keepdims=True)
    byte = np.maximum(np.where(amax > 0, np.frexp(amax)[1] - 1 + 127, 0) - down, 1)
    scale = np.exp2(byte - 127.0)
    codes = (blocks / scale).astype(np.float32).astype(dtype).astype(np.float64)
    return np.moveaxis((codes * scale).reshape(v.shape), -1, axis)


WIDE = False


def mx_kscale(k):
    if not WIDE:
        return np.ones(k)
    levels = np.array([10, -10, 5, -5, 0])
    if k % 512:
        return np.exp2(np.random.permutation(np.resize(levels, k // 32))).repeat(32)
    a = np.empty((k // 512, 16))
    for p in range(k // 512):
        a[p, :8] = np.random.permutation(np.resize(levels, 8))
        for g in range(8):
            far = levels[np.abs(levels - a[p, g]) >= 10]
            a[p, g + 8] = far[np.random.randint(len(far))]
    return np.exp2(a.ravel()).repeat(32)


def f64(x):
    return np.asarray(x).astype(np.float64)


def striped(idx):
    return np.tile(idx.reshape(-1, 16).T, (8, 1)).astype(np.uint16)


def unstriped(offs):
    return offs[:16].T.reshape(-1).astype(np.int64)


E2M1 = np.array([0.0, 0.5, 1.0, 1.5, 2.0, 3.0, 4.0, 6.0, -0.0, -0.5, -1.0, -1.5, -2.0, -3.0, -4.0, -6.0])


def pack_weight(w, fmt):
    k, n = w.shape
    w = f64(np.asarray(w, np.float32).astype(ml_dtypes.bfloat16)).reshape(k // 32, 32, n)
    amax = np.abs(w).max(1)
    if fmt == "e4m3":
        byte = np.frexp(amax)[1] - 1 + 127 - 7
    else:
        mant, ex = np.frexp(amax / 6.0)
        byte = np.where(mant > 0.5, ex, ex - 1) + 127
    byte = np.clip(np.where(amax > 0, byte, 1), 1, 254)
    scaled = (w * np.exp2(127.0 - byte)[:, None, :]).reshape(k, n).astype(np.float32)
    by_word = np.ascontiguousarray(scaled.reshape(k // 512, 128, 4, n).transpose(0, 1, 3, 2))
    if fmt == "e4m3":
        words = by_word.astype(ml_dtypes.float8_e4m3fn).view(np.uint8)
    else:
        c = by_word.astype(ml_dtypes.float4_e2m1fn).view(np.uint8) & 0xF
        words = (c[..., 0::2] | (c[..., 1::2] << 4)).reshape(k // 512, 128, 2 * n)
    return np.ascontiguousarray(words), np.ascontiguousarray(byte.astype(np.uint8).reshape(k // 512, 16, n))


def unpack_weight(words, scales, fmt):
    g, _, n = scales.shape
    words = np.ascontiguousarray(words).reshape(g, 128, n, -1)
    if fmt == "e4m3":
        vals = words.view(ml_dtypes.float8_e4m3fn).astype(np.float64)
    else:
        nib = np.empty((g, 128, n, 4), np.uint8)
        nib[..., 0::2] = words & 0xF
        nib[..., 1::2] = words >> 4
        vals = E2M1[nib]
    vals = vals * np.repeat(np.exp2(scales.astype(np.float64) - 127.0), 8, axis=1)[..., None]
    return vals.transpose(0, 1, 3, 2).reshape(g * 512, n)


def gelu(v):
    return 0.5 * v * (1.0 + np.tanh(np.sqrt(2.0 / np.pi) * (v + 0.044715 * v**3)))


K, T, S, H, N, T2 = 512, 4096, 1024, 1536, 768, 2048

def setup_inputs():
    n = np.random.standard_normal
    s = mx_kscale(K)[:, None]
    u = mx_kscale(H)[:, None]
    tab_words, tab_scales = pack_weight(n((K, T)) * s, "e4m3")
    wa_words, wa_scales = pack_weight(1.2 * n((K, H)) / np.sqrt(K) / s, "e2m1")
    return {
        "tab_words": tab_words, "tab_scales": tab_scales,
        "offs": striped(np.random.permutation(T)[:S]),
        "offs2": striped(np.random.permutation(T)[:S]),
        "offs3": striped(np.random.permutation(T2)[:S]),
        "wa_words": wa_words, "wa_scales": wa_scales,
        "ba": (0.8 * n(H)).astype(np.float32),
        "wb": (n((K, H)) / np.sqrt(K) / s).astype(np.float32),
        "gain": (np.exp(0.3 * n(H)) * u[:, 0]).astype(np.float32),
        "wc": (1.2 * n((H, N)) / np.sqrt(H) / u).astype(np.float32),
        "lam": np.exp(0.4 * n(N)).astype(np.float32),
        "wgo": np.exp(0.3 * n((128, S))).astype(np.float32),
    }

def reference(tab_words, tab_scales, offs, offs2, offs3, wa_words, wa_scales, ba, wb, gain, wc, lam, wgo):
    TW = unpack_weight(tab_words, tab_scales, "e4m3")
    v = TW[:, unstriped(offs)]
    v2 = TW[:, unstriped(offs2)]
    wa = unpack_weight(wa_words, wa_scales, "e2m1")
    have = np.tanh((wa.T @ v) + f64(ba)[:, None])
    need = mxq(f64(wb), 0, "e4m3").T @ v2
    h = (have + need) * f64(gain)[:, None]
    y = np.tanh(mxq(f64(wc), 0, "e4m3").T @ mxq(h, 0, "e4m3"))
    y = y * f64(lam)[:, None]
    out = np.zeros((N, T2))
    out[:, unstriped(offs3)] = np.tile(f64(wgo), (N // 128, 1)) * y
    return out

@@ -1,0 +1,250 @@
+from contextlib import ExitStack
+
+import concourse.mybir as mybir
+
+K, T, S, H, N, T2 = 512, 4096, 1024, 1536, 768, 2048
+FLOPS = 2 * S * (2 * K * H + H * N)
+
+F32 = mybir.dt.float32
+BF16 = mybir.dt.bfloat16
+I32 = mybir.dt.int32
+U32 = mybir.dt.uint32
+U16 = mybir.dt.uint16
+U8 = mybir.dt.uint8
+FP8X4 = mybir.dt.float8_e4m3fn_x4
+FP4X4 = mybir.dt.float4_e2m1fn_x4
+TANH = mybir.ActivationFunctionType.Tanh
+COPY = mybir.ActivationFunctionType.Copy
+ADD = mybir.AluOpType.add
+MULT = mybir.AluOpType.mult
+
+P = 128
+PACK = 4
+K_PASS = P * PACK
+HALF = 512
+CHUNK = 256
+N_CHUNKS = S // CHUNK
+H_PASSES = H // K_PASS
+N_TILES = N // P
+WC_HALF = N // 2
+WB_ON_SCALAR = (0,)
+WC_ON_SCALAR = (2,)
+PAGES_ON_VECTOR = 3
+HELD_PAGES = 2
+
+
+def tile_list_van_run_sheet_kernel(
+    tc, tab_words, tab_scales, offs, offs2, offs3, wa_words, wa_scales, ba, wb, gain, wc, lam, wgo, out
+):
+    nc = tc.nc
+    with ExitStack() as ctx:
+        lists = ctx.enter_context(tc.tile_pool(name="lists", bufs=1))
+        keep = ctx.enter_context(tc.tile_pool(name="keep", bufs=1))
+        stage = ctx.enter_context(tc.tile_pool(name="stage", bufs=1))
+        psum = ctx.enter_context(tc.psum_pool(name="psum", bufs=3))
+
+        idx = lists.tile([P, S // 16], U16, name="idx")
+        idx2 = lists.tile([P, S // 16], U16, name="idx2")
+        idx3 = lists.tile([P, S // 16], U16, name="idx3")
+
+        def load_scale_rows(queue, plane, rows):
+            for q in range(4):
+                queue.dma_start(
+                    out=plane[32 * q : 32 * q + 4, :].bitcast(I32),
+                    in_=rows[0, 4 * q : 4 * q + 4, :].bitcast(I32),
+                )
+
+        def round_copy(on_scalar, dst, src):
+            if on_scalar:
+                nc.scalar.copy(dst, src)
+            else:
+                nc.vector.tensor_copy(dst, src)
+
+        lam_cols = keep.tile([P, N_TILES], F32, name="lam_cols")
+        ba_cols = keep.tile([P, H_PASSES, PACK], F32, name="ba_cols")
+        gain_cols = keep.tile([P, H_PASSES, PACK], F32, name="gain_cols")
+        pages = [keep.tile([P, T2], F32, name="page%d" % i) for i in range(N_TILES)]
+        factor = [keep.tile([P, S], F32, name="factor%d" % i) for i in range(N_TILES)]
+        halves = S // HALF
+        v_codes = [[keep.tile([P, HALF], U32, name="v_codes%d%d" % (e, g), align_bytes=64) for g in range(halves)] for e in range(2)]
+        v_scales = [[keep.tile([P, HALF], U8, name="v_scales%d%d" % (e, g), align_bytes=64) for g in range(halves)] for e in range(2)]
+        wa_codes = [keep.tile([P, 2 * K_PASS], U8, name="wa_codes%d" % b, align_bytes=64) for b in range(H_PASSES)]
+        wa_plane = [keep.tile([P, K_PASS], U8, name="wa_plane%d" % b, align_bytes=64) for b in range(H_PASSES)]
+        wb_codes = [keep.tile([P, K_PASS], U32, name="wb_codes%d" % b, align_bytes=64) for b in range(H_PASSES)]
+        wb_plane = [keep.tile([P, K_PASS], U8, name="wb_plane%d" % b, align_bytes=64) for b in range(H_PASSES)]
+        wc_codes = [[keep.tile([P, WC_HALF], U32, name="wc_codes%d%d" % (b, u), align_bytes=64) for u in range(2)] for b in range(H_PASSES)]
+        wc_plane = [[keep.tile([P, WC_HALF], U8, name="wc_plane%d%d" % (b, u), align_bytes=64) for u in range(2)] for b in range(H_PASSES)]
+        wc_raw = [stage.tile([P, PACK, N], F32, name="wc_raw%d" % b) for b in range(H_PASSES)]
+
+        with tc.tile_pool(name="early", bufs=1) as early:
+            table_plane = early.tile([P, T], U8, name="table_plane")
+            table = early.tile([P, T], U32, name="table")
+            wa_raw = early.tile([P, 2 * H], U8, name="wa_raw")
+            wa_raw_plane = early.tile([P, H], U8, name="wa_raw_plane")
+            wgo_sb = early.tile([P, S], F32, name="wgo_sb")
+            wb_raw = [early.tile([P, PACK, K_PASS], F32, name="wb_raw%d" % b) for b in range(H_PASSES)]
+
+            nc.vector.memset(table_plane[:].bitcast(I32), 0)
+            nc.gpsimd.memset(wa_raw_plane[:].bitcast(I32), 0)
+            with nc.allow_non_contiguous_dma(reason="one value of lam a partition"):
+                nc.gpsimd.dma_start(out=lam_cols[:], in_=lam.rearrange("(i p) -> p i", p=P))
+            nc.gpsimd.dma_start(out=ba_cols[:], in_=ba.rearrange("(b p t) -> p b t", p=P, t=PACK))
+            nc.gpsimd.dma_start(out=gain_cols[:], in_=gain.rearrange("(b p t) -> p b t", p=P, t=PACK))
+            nc.sync.dma_start(idx[:], offs)
+            nc.sync.dma_start(out=wgo_sb[:], in_=wgo)
+            load_scale_rows(nc.sync, table_plane, tab_scales)
+            nc.sync.dma_start(out=wa_raw[:].bitcast(I32), in_=wa_words[0].bitcast(I32))
+            nc.sync.dma_start(out=table[:].bitcast(I32), in_=tab_words[0].rearrange("p t i -> p (t i)").bitcast(I32))
+            nc.sync.dma_start(idx2[:], offs2)
+            load_scale_rows(nc.sync, wa_raw_plane, wa_scales)
+            for b in range(H_PASSES):
+                nc.sync.dma_start(out=wb_raw[b][:], in_=wb[:, b * K_PASS : (b + 1) * K_PASS].rearrange("(p i) c -> p i c", i=PACK))
+            for b in range(H_PASSES):
+                nc.sync.dma_start(out=wc_raw[b][:], in_=wc[b * K_PASS : (b + 1) * K_PASS, :].rearrange("(p t) n -> p t n", t=PACK))
+            nc.sync.dma_start(idx3[:], offs3)
+
+            for i in range(PAGES_ON_VECTOR):
+                nc.vector.memset(pages[i][:], 0.0)
+            for i in range(PAGES_ON_VECTOR, N_TILES):
+                for c0 in range(0, T2, HALF):
+                    nc.gpsimd.memset(pages[i][:, c0 : c0 + HALF], 0.0)
+            for i in range(N_TILES):
+                nc.scalar.activation(factor[i][:], wgo_sb[:], COPY, scale=lam_cols[:, i : i + 1])
+
+            def gather(dst, window, e, g):
+                cols = slice(g * HALF // 16, (g + 1) * HALF // 16)
+                nc.vector.tensor_copy(dst[e][g][:], window[:].indirect((idx, idx2)[e][:, cols]))
+
+            for g in range(halves):
+                gather(v_scales, table_plane, 0, g)
+            for b in range(H_PASSES):
+                nc.vector.tensor_copy(
+                    wa_codes[b][:].bitcast(U16).rearrange("p (t m) -> p t m", t=PACK),
+                    wa_raw[:, 2 * b * K_PASS : 2 * (b + 1) * K_PASS].bitcast(U16).rearrange("p (m t) -> p t m", t=PACK),
+                )
+                nc.vector.tensor_copy(
+                    wa_plane[b][:].rearrange("p (t m) -> p t m", t=PACK),
+                    wa_raw_plane[:, b * K_PASS : (b + 1) * K_PASS].rearrange("p (m t) -> p t m", t=PACK),
+                )
+            gather(v_codes, table, 0, 0)
+            gather(v_scales, table_plane, 1, 0)
+            gather(v_codes, table, 1, 0)
+
+            for b in range(H_PASSES):
+                rounded = stage.tile([P, PACK * K_PASS], BF16, name="wb_rounded", tag="rounded", bufs=2, align_bytes=64)
+                round_copy(
+                    b in WB_ON_SCALAR,
+                    rounded[:].rearrange("p (t m i) -> p m i t", t=PACK, i=PACK),
+                    wb_raw[b][:].rearrange("p i (m t) -> p m i t", t=PACK),
+                )
+                nc.vector.quantize_mx(out=wb_codes[b][:].bitcast(FP8X4), scales=wb_plane[b][:], in_=rounded[:])
+            gather(v_codes, table, 0, 1)
+            gather(v_scales, table_plane, 1, 1)
+            gather(v_codes, table, 1, 1)
+
+        late = ctx.enter_context(tc.tile_pool(name="late", bufs=1))
+        h_codes = [[late.tile([P, HALF], U32, name="h_codes%d%d" % (g, b), align_bytes=64) for b in range(H_PASSES)] for g in range(halves)]
+        h_plane = [[late.tile([P, HALF], U8, name="h_plane%d%d" % (g, b), align_bytes=64) for b in range(H_PASSES)] for g in range(halves)]
+
+        def quantize_wc(b):
+            for u in range(2):
+                rounded = stage.tile([P, PACK * WC_HALF], BF16, name="wc_rounded", tag="rounded", bufs=2, align_bytes=64)
+                round_copy(
+                    b in WC_ON_SCALAR,
+                    rounded[:].rearrange("p (c e t) -> p c t e", t=PACK, e=2),
+                    wc_raw[b][:, :, u * WC_HALF : (u + 1) * WC_HALF].rearrange("p t (c e) -> p c t e", e=2),
+                )
+                nc.vector.quantize_mx(out=wc_codes[b][u][:].bitcast(FP8X4), scales=wc_plane[b][u][:], in_=rounded[:])
+
+        def first_stage(c, b):
+            g, lo = divmod(c * CHUNK, HALF)
+            cols = slice(lo, lo + CHUNK)
+            have = stage.tile([P, PACK, CHUNK], F32, name="have", bufs=4)
+            need = stage.tile([P, PACK, CHUNK], F32, name="need", bufs=4)
+            for t0 in range(0, PACK, 2):
+                acc = psum.tile([P, 2, CHUNK], F32, name="acc_have")
+                for s in range(2):
+                    m0 = (t0 + s) * P
+                    nc.tensor.matmul_mx(
+                        out=acc[:, s, :],
+                        lhsT=wa_codes[b][:, 2 * m0 : 2 * (m0 + P)].bitcast(FP4X4),
+                        lhsT_scale=wa_plane[b][:, m0 : m0 + P],
+                        rhs=v_codes[0][g][:, cols].bitcast(FP8X4),
+                        rhs_scale=v_scales[0][g][:, cols],
+                        start=True,
+                        stop=True,
+                    )
+                for s in range(2):
+                    t = t0 + s
+                    nc.scalar.activation(have[:, t, :], acc[:, s, :], TANH, bias=ba_cols[:, b, t : t + 1])
+            for t in range(PACK):
+                nc.scalar.activation(have[:, t, :], have[:, t, :], COPY, scale=gain_cols[:, b, t : t + 1])
+            for t0 in range(0, PACK, 2):
+                acc = psum.tile([P, 2, CHUNK], F32, name="acc_need")
+                for s in range(2):
+                    m0 = (t0 + s) * P
+                    nc.tensor.matmul_mx(
+                        out=acc[:, s, :],
+                        lhsT=wb_codes[b][:, m0 : m0 + P].bitcast(FP8X4),
+                        lhsT_scale=wb_plane[b][:, m0 : m0 + P],
+                        rhs=v_codes[1][g][:, cols].bitcast(FP8X4),
+                        rhs_scale=v_scales[1][g][:, cols],
+                        start=True,
+                        stop=True,
+                    )
+                for s in range(2):
+                    t = t0 + s
+                    nc.scalar.activation(need[:, t, :], acc[:, s, :], COPY, scale=gain_cols[:, b, t : t + 1])
+            h_rounded = late.tile([P, PACK * CHUNK], BF16, name="h_rounded", bufs=3, align_bytes=64)
+            nc.vector.tensor_tensor(
+                h_rounded[:].rearrange("p (c e t) -> p c t e", t=PACK, e=2),
+                have[:].rearrange("p t (c e) -> p c t e", e=2),
+                need[:].rearrange("p t (c e) -> p c t e", e=2),
+                ADD,
+            )
+            nc.vector.quantize_mx(out=h_codes[g][b][:, cols].bitcast(FP8X4), scales=h_plane[g][b][:, cols], in_=h_rounded[:])
+
+        def second_stage(j0, width, i):
+            g, lo = divmod(j0, HALF)
+            cols = slice(lo, lo + width)
+            u, m0 = divmod(i * P, WC_HALF)
+            acc = psum.tile([P, width], F32, name="acc_y", bufs=2)
+            for b in range(H_PASSES):
+                nc.tensor.matmul_mx(
+                    out=acc[:],
+                    lhsT=wc_codes[b][u][:, m0 : m0 + P].bitcast(FP8X4),
+                    lhsT_scale=wc_plane[b][u][:, m0 : m0 + P],
+                    rhs=h_codes[g][b][:, cols].bitcast(FP8X4),
+                    rhs_scale=h_plane[g][b][:, cols],
+                    start=(b == 0),
+                    stop=(b == H_PASSES - 1),
+                )
+            y = late.tile([P, width], F32, name="y", bufs=8)
+            nc.scalar.activation(y[:], acc[:], TANH)
+            nc.vector.tensor_tensor(
+                pages[i][:].indirect(idx3[:, j0 // 16 : (j0 + width) // 16]),
+                y[:],
+                factor[i][:, j0 : j0 + width],
+                MULT,
+            )
+            if j0 + width == S:
+                nc.sync.dma_start(out=out[i * P : (i + 1) * P, :], in_=pages[i][:])
+
+        for b in range(H_PASSES):
+            first_stage(0, b)
+        for b in range(H_PASSES):
+            quantize_wc(b)
+        for b in range(H_PASSES):
+            first_stage(1, b)
+        last = N_CHUNKS - 1
+        for c in range(last - 1):
+            for b in range(H_PASSES):
+                for i in range(2 * b, 2 * b + 2):
+                    second_stage(c * CHUNK, CHUNK, i)
+                first_stage(c + 2, b)
+        for i in range(N_TILES - HELD_PAGES):
+            second_stage((last - 1) * CHUNK, CHUNK, i)
+        for i in range(N_TILES - HELD_PAGES):
+            second_stage(last * CHUNK, CHUNK, i)
+        for i in range(N_TILES - HELD_PAGES, N_TILES):
+            second_stage((last - 1) * CHUNK, 2 * CHUNK, i)

@@ -28,8 +28,7 @@ H_PASSES = H // K_PASS
 N_TILES = N // P
 WC_HALF = N // 2
 WB_ON_SCALAR = (0,)
-WC_ON_SCALAR = (2,)
-PAGES_ON_VECTOR = 3
+WC_ON_SCALAR = (1, 2)
 HELD_PAGES = 2
 
 
@@ -66,8 +65,8 @@ def tile_list_van_run_sheet_kernel(
         pages = [keep.tile([P, T2], F32, name="page%d" % i) for i in range(N_TILES)]
         factor = [keep.tile([P, S], F32, name="factor%d" % i) for i in range(N_TILES)]
         halves = S // HALF
-        v_codes = [[keep.tile([P, HALF], U32, name="v_codes%d%d" % (e, g), align_bytes=64) for g in range(halves)] for e in range(2)]
-        v_scales = [[keep.tile([P, HALF], U8, name="v_scales%d%d" % (e, g), align_bytes=64) for g in range(halves)] for e in range(2)]
+        v_codes = {}
+        v_scales = {}
         wa_codes = [keep.tile([P, 2 * K_PASS], U8, name="wa_codes%d" % b, align_bytes=64) for b in range(H_PASSES)]
         wa_plane = [keep.tile([P, K_PASS], U8, name="wa_plane%d" % b, align_bytes=64) for b in range(H_PASSES)]
         wb_codes = [keep.tile([P, K_PASS], U32, name="wb_codes%d" % b, align_bytes=64) for b in range(H_PASSES)]
@@ -75,60 +74,65 @@ def tile_list_van_run_sheet_kernel(
         wc_codes = [[keep.tile([P, WC_HALF], U32, name="wc_codes%d%d" % (b, u), align_bytes=64) for u in range(2)] for b in range(H_PASSES)]
         wc_plane = [[keep.tile([P, WC_HALF], U8, name="wc_plane%d%d" % (b, u), align_bytes=64) for u in range(2)] for b in range(H_PASSES)]
         wc_raw = [stage.tile([P, PACK, N], F32, name="wc_raw%d" % b) for b in range(H_PASSES)]
+        wb_raw = [stage.tile([P, PACK, K_PASS], F32, name="wb_raw%d" % b, align_bytes=64) for b in range(H_PASSES)]
+        wa_raw_plane = stage.tile([P, H], U8, name="wa_raw_plane", align_bytes=64)
 
         with tc.tile_pool(name="early", bufs=1) as early:
             table_plane = early.tile([P, T], U8, name="table_plane")
             table = early.tile([P, T], U32, name="table")
             wa_raw = early.tile([P, 2 * H], U8, name="wa_raw")
-            wa_raw_plane = early.tile([P, H], U8, name="wa_raw_plane")
             wgo_sb = early.tile([P, S], F32, name="wgo_sb")
-            wb_raw = [early.tile([P, PACK, K_PASS], F32, name="wb_raw%d" % b) for b in range(H_PASSES)]
+
+            def load_wb(b):
+                nc.sync.dma_start(out=wb_raw[b][:], in_=wb[:, b * K_PASS : (b + 1) * K_PASS].rearrange("(p i) c -> p i c", i=PACK))
 
             nc.vector.memset(table_plane[:].bitcast(I32), 0)
-            nc.gpsimd.memset(wa_raw_plane[:].bitcast(I32), 0)
-            with nc.allow_non_contiguous_dma(reason="one value of lam a partition"):
-                nc.gpsimd.dma_start(out=lam_cols[:], in_=lam.rearrange("(i p) -> p i", p=P))
-            nc.gpsimd.dma_start(out=ba_cols[:], in_=ba.rearrange("(b p t) -> p b t", p=P, t=PACK))
-            nc.gpsimd.dma_start(out=gain_cols[:], in_=gain.rearrange("(b p t) -> p b t", p=P, t=PACK))
+            nc.vector.memset(wa_raw_plane[:].bitcast(I32), 0)
             nc.sync.dma_start(idx[:], offs)
+            with nc.allow_non_contiguous_dma(reason="one value of lam a partition"):
+                nc.sync.dma_start(out=lam_cols[:], in_=lam.rearrange("(i p) -> p i", p=P))
             nc.sync.dma_start(out=wgo_sb[:], in_=wgo)
-            load_scale_rows(nc.sync, table_plane, tab_scales)
-            nc.sync.dma_start(out=wa_raw[:].bitcast(I32), in_=wa_words[0].bitcast(I32))
-            nc.sync.dma_start(out=table[:].bitcast(I32), in_=tab_words[0].rearrange("p t i -> p (t i)").bitcast(I32))
+            nc.sync.dma_start(out=ba_cols[:], in_=ba.rearrange("(b p t) -> p b t", p=P, t=PACK))
+            nc.sync.dma_start(out=gain_cols[:], in_=gain.rearrange("(b p t) -> p b t", p=P, t=PACK))
             nc.sync.dma_start(idx2[:], offs2)
+            nc.sync.dma_start(idx3[:], offs3)
+            nc.sync.dma_start(out=table[:].bitcast(I32), in_=tab_words[0].rearrange("p t i -> p (t i)").bitcast(I32))
+            nc.sync.dma_start(out=wa_raw[:].bitcast(I32), in_=wa_words[0].bitcast(I32))
+            load_scale_rows(nc.sync, table_plane, tab_scales)
+            load_wb(0)
             load_scale_rows(nc.sync, wa_raw_plane, wa_scales)
-            for b in range(H_PASSES):
-                nc.sync.dma_start(out=wb_raw[b][:], in_=wb[:, b * K_PASS : (b + 1) * K_PASS].rearrange("(p i) c -> p i c", i=PACK))
+            for b in range(1, H_PASSES):
+                load_wb(b)
             for b in range(H_PASSES):
                 nc.sync.dma_start(out=wc_raw[b][:], in_=wc[b * K_PASS : (b + 1) * K_PASS, :].rearrange("(p t) n -> p t n", t=PACK))
-            nc.sync.dma_start(idx3[:], offs3)
 
-            for i in range(PAGES_ON_VECTOR):
+            for i in range(N_TILES):
                 nc.vector.memset(pages[i][:], 0.0)
-            for i in range(PAGES_ON_VECTOR, N_TILES):
-                for c0 in range(0, T2, HALF):
-                    nc.gpsimd.memset(pages[i][:, c0 : c0 + HALF], 0.0)
             for i in range(N_TILES):
                 nc.scalar.activation(factor[i][:], wgo_sb[:], COPY, scale=lam_cols[:, i : i + 1])
 
             def gather(dst, window, e, g):
                 cols = slice(g * HALF // 16, (g + 1) * HALF // 16)
-                nc.vector.tensor_copy(dst[e][g][:], window[:].indirect((idx, idx2)[e][:, cols]))
+                nc.vector.tensor_copy(dst, window[:].indirect((idx, idx2)[e][:, cols]))
+                return dst
 
-            for g in range(halves):
-                gather(v_scales, table_plane, 0, g)
+            def picked(dtype, width, tag):
+                return stage.tile([P, width], dtype, name="picked", tag=tag, align_bytes=64)
+
+            v_codes[0, 0] = gather(picked(U32, HALF, "codes00")[:], table, 0, 0)
             for b in range(H_PASSES):
                 nc.vector.tensor_copy(
                     wa_codes[b][:].bitcast(U16).rearrange("p (t m) -> p t m", t=PACK),
                     wa_raw[:, 2 * b * K_PASS : 2 * (b + 1) * K_PASS].bitcast(U16).rearrange("p (m t) -> p t m", t=PACK),
                 )
+            v_scales[0, 0] = gather(picked(U8, HALF, "scales00")[:], table_plane, 0, 0)
+            v_codes[1, 0] = gather(picked(U32, HALF, "codes10")[:], table, 1, 0)
+            for b in range(H_PASSES):
                 nc.vector.tensor_copy(
                     wa_plane[b][:].rearrange("p (t m) -> p t m", t=PACK),
                     wa_raw_plane[:, b * K_PASS : (b + 1) * K_PASS].rearrange("p (m t) -> p t m", t=PACK),
                 )
-            gather(v_codes, table, 0, 0)
-            gather(v_scales, table_plane, 1, 0)
-            gather(v_codes, table, 1, 0)
+            v_scales[1, 0] = gather(picked(U8, HALF, "wa_raw_plane")[:], table_plane, 1, 0)
 
             for b in range(H_PASSES):
                 rounded = stage.tile([P, PACK * K_PASS], BF16, name="wb_rounded", tag="rounded", bufs=2, align_bytes=64)
@@ -138,9 +142,11 @@ def tile_list_van_run_sheet_kernel(
                     wb_raw[b][:].rearrange("p i (m t) -> p m i t", t=PACK),
                 )
                 nc.vector.quantize_mx(out=wb_codes[b][:].bitcast(FP8X4), scales=wb_plane[b][:], in_=rounded[:])
-            gather(v_codes, table, 0, 1)
-            gather(v_scales, table_plane, 1, 1)
-            gather(v_codes, table, 1, 1)
+            v_codes[0, 1] = gather(picked(U32, HALF, "wb_raw0")[:], table, 0, 1)
+            both = picked(U8, 2 * HALF, "wb_raw1")
+            for e in range(2):
+                v_scales[e, 1] = gather(both[:, e * HALF : (e + 1) * HALF], table_plane, e, 1)
+            v_codes[1, 1] = gather(picked(U32, HALF, "wb_raw2")[:], table, 1, 1)
 
         late = ctx.enter_context(tc.tile_pool(name="late", bufs=1))
         h_codes = [[late.tile([P, HALF], U32, name="h_codes%d%d" % (g, b), align_bytes=64) for b in range(H_PASSES)] for g in range(halves)]
@@ -169,8 +175,8 @@ def tile_list_van_run_sheet_kernel(
                         out=acc[:, s, :],
                         lhsT=wa_codes[b][:, 2 * m0 : 2 * (m0 + P)].bitcast(FP4X4),
                         lhsT_scale=wa_plane[b][:, m0 : m0 + P],
-                        rhs=v_codes[0][g][:, cols].bitcast(FP8X4),
-                        rhs_scale=v_scales[0][g][:, cols],
+                        rhs=v_codes[0, g][:, cols].bitcast(FP8X4),
+                        rhs_scale=v_scales[0, g][:, cols],
                         start=True,
                         stop=True,
                     )
@@ -187,8 +193,8 @@ def tile_list_van_run_sheet_kernel(
                         out=acc[:, s, :],
                         lhsT=wb_codes[b][:, m0 : m0 + P].bitcast(FP8X4),
                         lhsT_scale=wb_plane[b][:, m0 : m0 + P],
-                        rhs=v_codes[1][g][:, cols].bitcast(FP8X4),
-                        rhs_scale=v_scales[1][g][:, cols],
+                        rhs=v_codes[1, g][:, cols].bitcast(FP8X4),
+                        rhs_scale=v_scales[1, g][:, cols],
                         start=True,
                         stop=True,
                     )
@@ -219,7 +225,7 @@ def tile_list_van_run_sheet_kernel(
                     start=(b == 0),
                     stop=(b == H_PASSES - 1),
                 )
-            y = late.tile([P, width], F32, name="y", bufs=8)
+            y = late.tile([P, width], F32, name="y", bufs=6)
             nc.scalar.activation(y[:], acc[:], TANH)
             nc.vector.tensor_tensor(
                 pages[i][:].indirect(idx3[:, j0 // 16 : (j0 + width) // 16]),

@@ -28,7 +28,8 @@ H_PASSES = H // K_PASS
 N_TILES = N // P
 WC_HALF = N // 2
 WB_ON_SCALAR = (0,)
-WC_ON_SCALAR = (1, 2)
+WC_ON_SCALAR = (2,)
+EARLY_PAGES = 3
 HELD_PAGES = 2
 
 
@@ -53,6 +54,10 @@ def tile_list_van_run_sheet_kernel(
                     in_=rows[0, 4 * q : 4 * q + 4, :].bitcast(I32),
                 )
 
+        def clear_on_gpsimd(page):
+            for c0 in range(0, T2, HALF):
+                nc.gpsimd.memset(page[:, c0 : c0 + HALF], 0.0)
+
         def round_copy(on_scalar, dst, src):
             if on_scalar:
                 nc.scalar.copy(dst, src)
@@ -62,7 +67,7 @@ def tile_list_van_run_sheet_kernel(
         lam_cols = keep.tile([P, N_TILES], F32, name="lam_cols")
         ba_cols = keep.tile([P, H_PASSES, PACK], F32, name="ba_cols")
         gain_cols = keep.tile([P, H_PASSES, PACK], F32, name="gain_cols")
-        pages = [keep.tile([P, T2], F32, name="page%d" % i) for i in range(N_TILES)]
+        pages = [keep.tile([P, T2], F32, name="page%d" % i) for i in range(EARLY_PAGES)]
         factor = [keep.tile([P, S], F32, name="factor%d" % i) for i in range(N_TILES)]
         halves = S // HALF
         v_codes = {}
@@ -80,34 +85,35 @@ def tile_list_van_run_sheet_kernel(
         with tc.tile_pool(name="early", bufs=1) as early:
             table_plane = early.tile([P, T], U8, name="table_plane")
             table = early.tile([P, T], U32, name="table")
-            wa_raw = early.tile([P, 2 * H], U8, name="wa_raw")
+            wa_raw = [early.tile([P, 2 * K_PASS], U8, name="wa_raw%d" % b) for b in range(H_PASSES)]
             wgo_sb = early.tile([P, S], F32, name="wgo_sb")
 
             def load_wb(b):
                 nc.sync.dma_start(out=wb_raw[b][:], in_=wb[:, b * K_PASS : (b + 1) * K_PASS].rearrange("(p i) c -> p i c", i=PACK))
 
             nc.vector.memset(table_plane[:].bitcast(I32), 0)
-            nc.vector.memset(wa_raw_plane[:].bitcast(I32), 0)
+            nc.gpsimd.memset(wa_raw_plane[:].bitcast(I32), 0)
             nc.sync.dma_start(idx[:], offs)
-            with nc.allow_non_contiguous_dma(reason="one value of lam a partition"):
-                nc.sync.dma_start(out=lam_cols[:], in_=lam.rearrange("(i p) -> p i", p=P))
-            nc.sync.dma_start(out=wgo_sb[:], in_=wgo)
-            nc.sync.dma_start(out=ba_cols[:], in_=ba.rearrange("(b p t) -> p b t", p=P, t=PACK))
-            nc.sync.dma_start(out=gain_cols[:], in_=gain.rearrange("(b p t) -> p b t", p=P, t=PACK))
             nc.sync.dma_start(idx2[:], offs2)
             nc.sync.dma_start(idx3[:], offs3)
-            nc.sync.dma_start(out=table[:].bitcast(I32), in_=tab_words[0].rearrange("p t i -> p (t i)").bitcast(I32))
-            nc.sync.dma_start(out=wa_raw[:].bitcast(I32), in_=wa_words[0].bitcast(I32))
+            nc.sync.dma_start(out=ba_cols[:], in_=ba.rearrange("(b p t) -> p b t", p=P, t=PACK))
+            nc.sync.dma_start(out=gain_cols[:], in_=gain.rearrange("(b p t) -> p b t", p=P, t=PACK))
+            with nc.allow_non_contiguous_dma(reason="one value of lam a partition"):
+                nc.sync.dma_start(out=lam_cols[:], in_=lam.rearrange("(i p) -> p i", p=P))
+            for b in range(H_PASSES):
+                nc.sync.dma_start(out=wa_raw[b][:].bitcast(I32), in_=wa_words[0, :, 2 * b * K_PASS : 2 * (b + 1) * K_PASS].bitcast(I32))
+            nc.sync.dma_start(out=wgo_sb[:], in_=wgo)
             load_scale_rows(nc.sync, table_plane, tab_scales)
-            load_wb(0)
+            nc.sync.dma_start(out=table[:].bitcast(I32), in_=tab_words[0].rearrange("p t i -> p (t i)").bitcast(I32))
             load_scale_rows(nc.sync, wa_raw_plane, wa_scales)
-            for b in range(1, H_PASSES):
+            for b in range(H_PASSES):
                 load_wb(b)
             for b in range(H_PASSES):
                 nc.sync.dma_start(out=wc_raw[b][:], in_=wc[b * K_PASS : (b + 1) * K_PASS, :].rearrange("(p t) n -> p t n", t=PACK))
 
-            for i in range(N_TILES):
-                nc.vector.memset(pages[i][:], 0.0)
+            nc.vector.memset(pages[0][:], 0.0)
+            for i in range(1, EARLY_PAGES):
+                clear_on_gpsimd(pages[i])
             for i in range(N_TILES):
                 nc.scalar.activation(factor[i][:], wgo_sb[:], COPY, scale=lam_cols[:, i : i + 1])
 
@@ -119,33 +125,32 @@ def tile_list_van_run_sheet_kernel(
             def picked(dtype, width, tag):
                 return stage.tile([P, width], dtype, name="picked", tag=tag, align_bytes=64)
 
-            v_codes[0, 0] = gather(picked(U32, HALF, "codes00")[:], table, 0, 0)
             for b in range(H_PASSES):
                 nc.vector.tensor_copy(
                     wa_codes[b][:].bitcast(U16).rearrange("p (t m) -> p t m", t=PACK),
-                    wa_raw[:, 2 * b * K_PASS : 2 * (b + 1) * K_PASS].bitcast(U16).rearrange("p (m t) -> p t m", t=PACK),
+                    wa_raw[b][:].bitcast(U16).rearrange("p (m t) -> p t m", t=PACK),
                 )
             v_scales[0, 0] = gather(picked(U8, HALF, "scales00")[:], table_plane, 0, 0)
-            v_codes[1, 0] = gather(picked(U32, HALF, "codes10")[:], table, 1, 0)
+            v_scales[1, 0] = gather(picked(U8, HALF, "scales10")[:], table_plane, 1, 0)
+            v_scales[0, 1] = gather(picked(U8, HALF, "scales01")[:], table_plane, 0, 1)
+            v_codes[0, 0] = gather(picked(U32, HALF, "codes00")[:], table, 0, 0)
             for b in range(H_PASSES):
                 nc.vector.tensor_copy(
                     wa_plane[b][:].rearrange("p (t m) -> p t m", t=PACK),
                     wa_raw_plane[:, b * K_PASS : (b + 1) * K_PASS].rearrange("p (m t) -> p t m", t=PACK),
                 )
-            v_scales[1, 0] = gather(picked(U8, HALF, "wa_raw_plane")[:], table_plane, 1, 0)
+            v_codes[1, 0] = gather(picked(U32, HALF, "wa_raw_plane")[:], table, 1, 0)
 
             for b in range(H_PASSES):
                 rounded = stage.tile([P, PACK * K_PASS], BF16, name="wb_rounded", tag="rounded", bufs=2, align_bytes=64)
                 round_copy(
                     b in WB_ON_SCALAR,
-                    rounded[:].rearrange("p (t m i) -> p m i t", t=PACK, i=PACK),
-                    wb_raw[b][:].rearrange("p i (m t) -> p m i t", t=PACK),
+                    rounded[:].rearrange("p (u e m i) -> p u m i e", u=2, e=2, i=PACK),
+                    wb_raw[b][:].rearrange("p i (m u e) -> p u m i e", u=2, e=2),
                 )
                 nc.vector.quantize_mx(out=wb_codes[b][:].bitcast(FP8X4), scales=wb_plane[b][:], in_=rounded[:])
             v_codes[0, 1] = gather(picked(U32, HALF, "wb_raw0")[:], table, 0, 1)
-            both = picked(U8, 2 * HALF, "wb_raw1")
-            for e in range(2):
-                v_scales[e, 1] = gather(both[:, e * HALF : (e + 1) * HALF], table_plane, e, 1)
+            v_scales[1, 1] = gather(picked(U8, HALF, "wb_raw1")[:], table_plane, 1, 1)
             v_codes[1, 1] = gather(picked(U32, HALF, "wb_raw2")[:], table, 1, 1)
 
         late = ctx.enter_context(tc.tile_pool(name="late", bufs=1))
@@ -154,7 +159,11 @@ def tile_list_van_run_sheet_kernel(
 
         def quantize_wc(b):
             for u in range(2):
-                rounded = stage.tile([P, PACK * WC_HALF], BF16, name="wc_rounded", tag="rounded", bufs=2, align_bytes=64)
+                i = 2 * b + u
+                if i < EARLY_PAGES:
+                    rounded = stage.tile([P, PACK * WC_HALF], BF16, name="wc_rounded", tag="rounded", bufs=2, align_bytes=64)
+                else:
+                    rounded = keep.tile([P, PACK * WC_HALF], BF16, name="wc_rounded", tag="page%d" % i, align_bytes=64)
                 round_copy(
                     b in WC_ON_SCALAR,
                     rounded[:].rearrange("p (c e t) -> p c t e", t=PACK, e=2),
@@ -240,16 +249,19 @@ def tile_list_van_run_sheet_kernel(
             first_stage(0, b)
         for b in range(H_PASSES):
             quantize_wc(b)
-        for b in range(H_PASSES):
-            first_stage(1, b)
+        for i in range(EARLY_PAGES, N_TILES):
+            page = keep.tile([P, T2], F32, name="page%d" % i, align_bytes=64)
+            clear_on_gpsimd(page)
+            pages.append(page)
         last = N_CHUNKS - 1
-        for c in range(last - 1):
+        for c in range(last):
+            tiles = list(range(N_TILES if c < last - 1 else N_TILES - HELD_PAGES))
             for b in range(H_PASSES):
-                for i in range(2 * b, 2 * b + 2):
+                first_stage(c + 1, b)
+                count = len(tiles) - 2 * (H_PASSES - 1 - b)
+                for i in tiles[:count]:
                     second_stage(c * CHUNK, CHUNK, i)
-                first_stage(c + 2, b)
-        for i in range(N_TILES - HELD_PAGES):
-            second_stage((last - 1) * CHUNK, CHUNK, i)
+                tiles = tiles[count:]
         for i in range(N_TILES - HELD_PAGES):
             second_stage(last * CHUNK, CHUNK, i)
         for i in range(N_TILES - HELD_PAGES, N_TILES):

@@ -22,6 +22,7 @@ P = 128
 PACK = 4
 K_PASS = P * PACK
 HALF = 512
+RUN = 4
 CHUNK = 256
 N_CHUNKS = S // CHUNK
 H_PASSES = H // K_PASS
@@ -96,24 +97,26 @@ def tile_list_van_run_sheet_kernel(
             nc.sync.dma_start(idx[:], offs)
             nc.sync.dma_start(idx2[:], offs2)
             nc.sync.dma_start(idx3[:], offs3)
-            nc.sync.dma_start(out=ba_cols[:], in_=ba.rearrange("(b p t) -> p b t", p=P, t=PACK))
-            nc.sync.dma_start(out=gain_cols[:], in_=gain.rearrange("(b p t) -> p b t", p=P, t=PACK))
             with nc.allow_non_contiguous_dma(reason="one value of lam a partition"):
                 nc.sync.dma_start(out=lam_cols[:], in_=lam.rearrange("(i p) -> p i", p=P))
             for b in range(H_PASSES):
                 nc.sync.dma_start(out=wa_raw[b][:].bitcast(I32), in_=wa_words[0, :, 2 * b * K_PASS : 2 * (b + 1) * K_PASS].bitcast(I32))
-            nc.sync.dma_start(out=wgo_sb[:], in_=wgo)
+            for c0 in range(0, S, HALF):
+                nc.sync.dma_start(out=wgo_sb[:, c0 : c0 + HALF], in_=wgo[:, c0 : c0 + HALF])
             load_scale_rows(nc.sync, table_plane, tab_scales)
             nc.sync.dma_start(out=table[:].bitcast(I32), in_=tab_words[0].rearrange("p t i -> p (t i)").bitcast(I32))
             load_scale_rows(nc.sync, wa_raw_plane, wa_scales)
-            for b in range(H_PASSES):
+            load_wb(0)
+            nc.sync.dma_start(out=ba_cols[:], in_=ba.rearrange("(b p t) -> p b t", p=P, t=PACK))
+            nc.sync.dma_start(out=gain_cols[:], in_=gain.rearrange("(b p t) -> p b t", p=P, t=PACK))
+            for b in range(1, H_PASSES):
                 load_wb(b)
             for b in range(H_PASSES):
                 nc.sync.dma_start(out=wc_raw[b][:], in_=wc[b * K_PASS : (b + 1) * K_PASS, :].rearrange("(p t) n -> p t n", t=PACK))
 
-            nc.vector.memset(pages[0][:], 0.0)
-            for i in range(1, EARLY_PAGES):
-                clear_on_gpsimd(pages[i])
+            for i in range(EARLY_PAGES - 1):
+                nc.vector.memset(pages[i][:], 0.0)
+            clear_on_gpsimd(pages[EARLY_PAGES - 1])
             for i in range(N_TILES):
                 nc.scalar.activation(factor[i][:], wgo_sb[:], COPY, scale=lam_cols[:, i : i + 1])
 
@@ -166,16 +169,16 @@ def tile_list_van_run_sheet_kernel(
                     rounded = keep.tile([P, PACK * WC_HALF], BF16, name="wc_rounded", tag="page%d" % i, align_bytes=64)
                 round_copy(
                     b in WC_ON_SCALAR,
-                    rounded[:].rearrange("p (c e t) -> p c t e", t=PACK, e=2),
-                    wc_raw[b][:, :, u * WC_HALF : (u + 1) * WC_HALF].rearrange("p t (c e) -> p c t e", e=2),
+                    rounded[:].rearrange("p (c e t) -> p c t e", t=PACK, e=RUN),
+                    wc_raw[b][:, :, u * WC_HALF : (u + 1) * WC_HALF].rearrange("p t (c e) -> p c t e", e=RUN),
                 )
                 nc.vector.quantize_mx(out=wc_codes[b][u][:].bitcast(FP8X4), scales=wc_plane[b][u][:], in_=rounded[:])
 
         def first_stage(c, b):
             g, lo = divmod(c * CHUNK, HALF)
             cols = slice(lo, lo + CHUNK)
-            have = stage.tile([P, PACK, CHUNK], F32, name="have", bufs=4)
-            need = stage.tile([P, PACK, CHUNK], F32, name="need", bufs=4)
+            have = stage.tile([P, CHUNK // RUN, PACK, RUN], F32, name="have", bufs=4)
+            need = stage.tile([P, CHUNK // RUN, PACK, RUN], F32, name="need", bufs=4)
             for t0 in range(0, PACK, 2):
                 acc = psum.tile([P, 2, CHUNK], F32, name="acc_have")
                 for s in range(2):
@@ -191,9 +194,9 @@ def tile_list_van_run_sheet_kernel(
                     )
                 for s in range(2):
                     t = t0 + s
-                    nc.scalar.activation(have[:, t, :], acc[:, s, :], TANH, bias=ba_cols[:, b, t : t + 1])
+                    nc.scalar.activation(have[:, :, t, :], acc[:, s, :].rearrange("p (c e) -> p c e", e=RUN), TANH, bias=ba_cols[:, b, t : t + 1])
             for t in range(PACK):
-                nc.scalar.activation(have[:, t, :], have[:, t, :], COPY, scale=gain_cols[:, b, t : t + 1])
+                nc.scalar.activation(have[:, :, t, :], have[:, :, t, :], COPY, scale=gain_cols[:, b, t : t + 1])
             for t0 in range(0, PACK, 2):
                 acc = psum.tile([P, 2, CHUNK], F32, name="acc_need")
                 for s in range(2):
@@ -209,12 +212,12 @@ def tile_list_van_run_sheet_kernel(
                     )
                 for s in range(2):
                     t = t0 + s
-                    nc.scalar.activation(need[:, t, :], acc[:, s, :], COPY, scale=gain_cols[:, b, t : t + 1])
+                    nc.scalar.activation(need[:, :, t, :], acc[:, s, :].rearrange("p (c e) -> p c e", e=RUN), COPY, scale=gain_cols[:, b, t : t + 1])
             h_rounded = late.tile([P, PACK * CHUNK], BF16, name="h_rounded", bufs=3, align_bytes=64)
             nc.vector.tensor_tensor(
-                h_rounded[:].rearrange("p (c e t) -> p c t e", t=PACK, e=2),
-                have[:].rearrange("p t (c e) -> p c t e", e=2),
-                need[:].rearrange("p t (c e) -> p c t e", e=2),
+                h_rounded[:].rearrange("p (c e t) -> p c t e", t=PACK, e=RUN),
+                have[:],
+                need[:],
                 ADD,
             )
             nc.vector.quantize_mx(out=h_codes[g][b][:, cols].bitcast(FP8X4), scales=h_plane[g][b][:, cols], in_=h_rounded[:])

from contextlib import ExitStack

import concourse.mybir as mybir

K, T, S, H, N, T2 = 512, 4096, 1024, 1536, 768, 2048
FLOPS = 2 * S * (2 * K * H + H * N)

F32 = mybir.dt.float32
BF16 = mybir.dt.bfloat16
I32 = mybir.dt.int32
U32 = mybir.dt.uint32
U16 = mybir.dt.uint16
U8 = mybir.dt.uint8
FP8X4 = mybir.dt.float8_e4m3fn_x4
FP4X4 = mybir.dt.float4_e2m1fn_x4
TANH = mybir.ActivationFunctionType.Tanh
COPY = mybir.ActivationFunctionType.Copy
ADD = mybir.AluOpType.add
MULT = mybir.AluOpType.mult

P = 128
PACK = 4
K_PASS = P * PACK
HALF = 512
RUN = 4
CHUNK = 256
N_CHUNKS = S // CHUNK
H_PASSES = H // K_PASS
N_TILES = N // P
WC_HALF = N // 2
WB_ON_SCALAR = (0,)
WC_ON_SCALAR = (2,)
EARLY_PAGES = 3
HELD_PAGES = 2


def tile_list_van_run_sheet_kernel(
    tc, tab_words, tab_scales, offs, offs2, offs3, wa_words, wa_scales, ba, wb, gain, wc, lam, wgo, out
):
    nc = tc.nc
    with ExitStack() as ctx:
        lists = ctx.enter_context(tc.tile_pool(name="lists", bufs=1))
        keep = ctx.enter_context(tc.tile_pool(name="keep", bufs=1))
        stage = ctx.enter_context(tc.tile_pool(name="stage", bufs=1))
        psum = ctx.enter_context(tc.psum_pool(name="psum", bufs=3))

        idx = lists.tile([P, S // 16], U16, name="idx")
        idx2 = lists.tile([P, S // 16], U16, name="idx2")
        idx3 = lists.tile([P, S // 16], U16, name="idx3")

        def load_scale_rows(queue, plane, rows):
            for q in range(4):
                queue.dma_start(
                    out=plane[32 * q : 32 * q + 4, :].bitcast(I32),
                    in_=rows[0, 4 * q : 4 * q + 4, :].bitcast(I32),
                )

        def clear_on_gpsimd(page):
            for c0 in range(0, T2, HALF):
                nc.gpsimd.memset(page[:, c0 : c0 + HALF], 0.0)

        def round_copy(on_scalar, dst, src):
            if on_scalar:
                nc.scalar.copy(dst, src)
            else:
                nc.vector.tensor_copy(dst, src)

        lam_cols = keep.tile([P, N_TILES], F32, name="lam_cols")
        ba_cols = keep.tile([P, H_PASSES, PACK], F32, name="ba_cols")
        gain_cols = keep.tile([P, H_PASSES, PACK], F32, name="gain_cols")
        pages = [keep.tile([P, T2], F32, name="page%d" % i) for i in range(EARLY_PAGES)]
        factor = [keep.tile([P, S], F32, name="factor%d" % i) for i in range(N_TILES)]
        halves = S // HALF
        v_codes = {}
        v_scales = {}
        wa_codes = [keep.tile([P, 2 * K_PASS], U8, name="wa_codes%d" % b, align_bytes=64) for b in range(H_PASSES)]
        wa_plane = [keep.tile([P, K_PASS], U8, name="wa_plane%d" % b, align_bytes=64) for b in range(H_PASSES)]
        wb_codes = [keep.tile([P, K_PASS], U32, name="wb_codes%d" % b, align_bytes=64) for b in range(H_PASSES)]
        wb_plane = [keep.tile([P, K_PASS], U8, name="wb_plane%d" % b, align_bytes=64) for b in range(H_PASSES)]
        wc_codes = [[keep.tile([P, WC_HALF], U32, name="wc_codes%d%d" % (b, u), align_bytes=64) for u in range(2)] for b in range(H_PASSES)]
        wc_plane = [[keep.tile([P, WC_HALF], U8, name="wc_plane%d%d" % (b, u), align_bytes=64) for u in range(2)] for b in range(H_PASSES)]
        wc_raw = [stage.tile([P, PACK, N], F32, name="wc_raw%d" % b) for b in range(H_PASSES)]
        wb_raw = [stage.tile([P, PACK, K_PASS], F32, name="wb_raw%d" % b, align_bytes=64) for b in range(H_PASSES)]
        wa_raw_plane = stage.tile([P, H], U8, name="wa_raw_plane", align_bytes=64)

        with tc.tile_pool(name="early", bufs=1) as early:
            table_plane = early.tile([P, T], U8, name="table_plane")
            table = early.tile([P, T], U32, name="table")
            wa_raw = [early.tile([P, 2 * K_PASS], U8, name="wa_raw%d" % b) for b in range(H_PASSES)]
            wgo_sb = early.tile([P, S], F32, name="wgo_sb")

            def load_wb(b):
                nc.sync.dma_start(out=wb_raw[b][:], in_=wb[:, b * K_PASS : (b + 1) * K_PASS].rearrange("(p i) c -> p i c", i=PACK))

            nc.vector.memset(table_plane[:].bitcast(I32), 0)
            nc.gpsimd.memset(wa_raw_plane[:].bitcast(I32), 0)
            nc.sync.dma_start(idx[:], offs)
            nc.sync.dma_start(idx2[:], offs2)
            nc.sync.dma_start(idx3[:], offs3)
            with nc.allow_non_contiguous_dma(reason="one value of lam a partition"):
                nc.sync.dma_start(out=lam_cols[:], in_=lam.rearrange("(i p) -> p i", p=P))
            for b in range(H_PASSES):
                nc.sync.dma_start(out=wa_raw[b][:].bitcast(I32), in_=wa_words[0, :, 2 * b * K_PASS : 2 * (b + 1) * K_PASS].bitcast(I32))
            for c0 in range(0, S, HALF):
                nc.sync.dma_start(out=wgo_sb[:, c0 : c0 + HALF], in_=wgo[:, c0 : c0 + HALF])
            load_scale_rows(nc.sync, table_plane, tab_scales)
            nc.sync.dma_start(out=table[:].bitcast(I32), in_=tab_words[0].rearrange("p t i -> p (t i)").bitcast(I32))
            load_scale_rows(nc.sync, wa_raw_plane, wa_scales)
            load_wb(0)
            nc.sync.dma_start(out=ba_cols[:], in_=ba.rearrange("(b p t) -> p b t", p=P, t=PACK))
            nc.sync.dma_start(out=gain_cols[:], in_=gain.rearrange("(b p t) -> p b t", p=P, t=PACK))
            for b in range(1, H_PASSES):
                load_wb(b)
            for b in range(H_PASSES):
                nc.sync.dma_start(out=wc_raw[b][:], in_=wc[b * K_PASS : (b + 1) * K_PASS, :].rearrange("(p t) n -> p t n", t=PACK))

            for i in range(EARLY_PAGES - 1):
                nc.vector.memset(pages[i][:], 0.0)
            clear_on_gpsimd(pages[EARLY_PAGES - 1])
            for i in range(N_TILES):
                nc.scalar.activation(factor[i][:], wgo_sb[:], COPY, scale=lam_cols[:, i : i + 1])

            def gather(dst, window, e, g):
                cols = slice(g * HALF // 16, (g + 1) * HALF // 16)
                nc.vector.tensor_copy(dst, window[:].indirect((idx, idx2)[e][:, cols]))
                return dst

            def picked(dtype, width, tag):
                return stage.tile([P, width], dtype, name="picked", tag=tag, align_bytes=64)

            for b in range(H_PASSES):
                nc.vector.tensor_copy(
                    wa_codes[b][:].bitcast(U16).rearrange("p (t m) -> p t m", t=PACK),
                    wa_raw[b][:].bitcast(U16).rearrange("p (m t) -> p t m", t=PACK),
                )
            v_scales[0, 0] = gather(picked(U8, HALF, "scales00")[:], table_plane, 0, 0)
            v_scales[1, 0] = gather(picked(U8, HALF, "scales10")[:], table_plane, 1, 0)
            v_scales[0, 1] = gather(picked(U8, HALF, "scales01")[:], table_plane, 0, 1)
            v_codes[0, 0] = gather(picked(U32, HALF, "codes00")[:], table, 0, 0)
            for b in range(H_PASSES):
                nc.vector.tensor_copy(
                    wa_plane[b][:].rearrange("p (t m) -> p t m", t=PACK),
                    wa_raw_plane[:, b * K_PASS : (b + 1) * K_PASS].rearrange("p (m t) -> p t m", t=PACK),
                )
            v_codes[1, 0] = gather(picked(U32, HALF, "wa_raw_plane")[:], table, 1, 0)

            for b in range(H_PASSES):
                rounded = stage.tile([P, PACK * K_PASS], BF16, name="wb_rounded", tag="rounded", bufs=2, align_bytes=64)
                round_copy(
                    b in WB_ON_SCALAR,
                    rounded[:].rearrange("p (u e m i) -> p u m i e", u=2, e=2, i=PACK),
                    wb_raw[b][:].rearrange("p i (m u e) -> p u m i e", u=2, e=2),
                )
                nc.vector.quantize_mx(out=wb_codes[b][:].bitcast(FP8X4), scales=wb_plane[b][:], in_=rounded[:])
            v_codes[0, 1] = gather(picked(U32, HALF, "wb_raw0")[:], table, 0, 1)
            v_scales[1, 1] = gather(picked(U8, HALF, "wb_raw1")[:], table_plane, 1, 1)
            v_codes[1, 1] = gather(picked(U32, HALF, "wb_raw2")[:], table, 1, 1)

        late = ctx.enter_context(tc.tile_pool(name="late", bufs=1))
        h_codes = [[late.tile([P, HALF], U32, name="h_codes%d%d" % (g, b), align_bytes=64) for b in range(H_PASSES)] for g in range(halves)]
        h_plane = [[late.tile([P, HALF], U8, name="h_plane%d%d" % (g, b), align_bytes=64) for b in range(H_PASSES)] for g in range(halves)]

        def quantize_wc(b):
            for u in range(2):
                i = 2 * b + u
                if i < EARLY_PAGES:
                    rounded = stage.tile([P, PACK * WC_HALF], BF16, name="wc_rounded", tag="rounded", bufs=2, align_bytes=64)
                else:
                    rounded = keep.tile([P, PACK * WC_HALF], BF16, name="wc_rounded", tag="page%d" % i, align_bytes=64)
                round_copy(
                    b in WC_ON_SCALAR,
                    rounded[:].rearrange("p (c e t) -> p c t e", t=PACK, e=RUN),
                    wc_raw[b][:, :, u * WC_HALF : (u + 1) * WC_HALF].rearrange("p t (c e) -> p c t e", e=RUN),
                )
                nc.vector.quantize_mx(out=wc_codes[b][u][:].bitcast(FP8X4), scales=wc_plane[b][u][:], in_=rounded[:])

        def first_stage(c, b):
            g, lo = divmod(c * CHUNK, HALF)
            cols = slice(lo, lo + CHUNK)
            have = stage.tile([P, CHUNK // RUN, PACK, RUN], F32, name="have", bufs=4)
            need = stage.tile([P, CHUNK // RUN, PACK, RUN], F32, name="need", bufs=4)
            for t0 in range(0, PACK, 2):
                acc = psum.tile([P, 2, CHUNK], F32, name="acc_have")
                for s in range(2):
                    m0 = (t0 + s) * P
                    nc.tensor.matmul_mx(
                        out=acc[:, s, :],
                        lhsT=wa_codes[b][:, 2 * m0 : 2 * (m0 + P)].bitcast(FP4X4),
                        lhsT_scale=wa_plane[b][:, m0 : m0 + P],
                        rhs=v_codes[0, g][:, cols].bitcast(FP8X4),
                        rhs_scale=v_scales[0, g][:, cols],
                        start=True,
                        stop=True,
                    )
                for s in range(2):
                    t = t0 + s
                    nc.scalar.activation(have[:, :, t, :], acc[:, s, :].rearrange("p (c e) -> p c e", e=RUN), TANH, bias=ba_cols[:, b, t : t + 1])
            for t in range(PACK):
                nc.scalar.activation(have[:, :, t, :], have[:, :, t, :], COPY, scale=gain_cols[:, b, t : t + 1])
            for t0 in range(0, PACK, 2):
                acc = psum.tile([P, 2, CHUNK], F32, name="acc_need")
                for s in range(2):
                    m0 = (t0 + s) * P
                    nc.tensor.matmul_mx(
                        out=acc[:, s, :],
                        lhsT=wb_codes[b][:, m0 : m0 + P].bitcast(FP8X4),
                        lhsT_scale=wb_plane[b][:, m0 : m0 + P],
                        rhs=v_codes[1, g][:, cols].bitcast(FP8X4),
                        rhs_scale=v_scales[1, g][:, cols],
                        start=True,
                        stop=True,
                    )
                for s in range(2):
                    t = t0 + s
                    nc.scalar.activation(need[:, :, t, :], acc[:, s, :].rearrange("p (c e) -> p c e", e=RUN), COPY, scale=gain_cols[:, b, t : t + 1])
            h_rounded = late.tile([P, PACK * CHUNK], BF16, name="h_rounded", bufs=3, align_bytes=64)
            nc.vector.tensor_tensor(
                h_rounded[:].rearrange("p (c e t) -> p c t e", t=PACK, e=RUN),
                have[:],
                need[:],
                ADD,
            )
            nc.vector.quantize_mx(out=h_codes[g][b][:, cols].bitcast(FP8X4), scales=h_plane[g][b][:, cols], in_=h_rounded[:])

        def second_stage(j0, width, i):
            g, lo = divmod(j0, HALF)
            cols = slice(lo, lo + width)
            u, m0 = divmod(i * P, WC_HALF)
            acc = psum.tile([P, width], F32, name="acc_y", bufs=2)
            for b in range(H_PASSES):
                nc.tensor.matmul_mx(
                    out=acc[:],
                    lhsT=wc_codes[b][u][:, m0 : m0 + P].bitcast(FP8X4),
                    lhsT_scale=wc_plane[b][u][:, m0 : m0 + P],
                    rhs=h_codes[g][b][:, cols].bitcast(FP8X4),
                    rhs_scale=h_plane[g][b][:, cols],
                    start=(b == 0),
                    stop=(b == H_PASSES - 1),
                )
            y = late.tile([P, width], F32, name="y", bufs=6)
            nc.scalar.activation(y[:], acc[:], TANH)
            nc.vector.tensor_tensor(
                pages[i][:].indirect(idx3[:, j0 // 16 : (j0 + width) // 16]),
                y[:],
                factor[i][:, j0 : j0 + width],
                MULT,
            )
            if j0 + width == S:
                nc.sync.dma_start(out=out[i * P : (i + 1) * P, :], in_=pages[i][:])

        for b in range(H_PASSES):
            first_stage(0, b)
        for b in range(H_PASSES):
            quantize_wc(b)
        for i in range(EARLY_PAGES, N_TILES):
            page = keep.tile([P, T2], F32, name="page%d" % i, align_bytes=64)
            clear_on_gpsimd(page)
            pages.append(page)
        last = N_CHUNKS - 1
        for c in range(last):
            tiles = list(range(N_TILES if c < last - 1 else N_TILES - HELD_PAGES))
            for b in range(H_PASSES):
                first_stage(c + 1, b)
                count = len(tiles) - 2 * (H_PASSES - 1 - b)
                for i in tiles[:count]:
                    second_stage(c * CHUNK, CHUNK, i)
                tiles = tiles[count:]
        for i in range(N_TILES - HELD_PAGES):
            second_stage(last * CHUNK, CHUNK, i)
        for i in range(N_TILES - HELD_PAGES, N_TILES):
            second_stage((last - 1) * CHUNK, 2 * CHUNK, i)
